import numpy as np, ml_dtypes
CORES = [40,64,80,88,96,104,120,144]
N = 8
import mx_ref
BF = ml_dtypes.bfloat16
def entries(a):
    return np.ascontiguousarray(a.T).reshape(-1)
def table(e):
    return np.ascontiguousarray(np.reshape(e, (-1, 16)).T).astype(np.int32)
def cut(t, i, w=512):
    return t[:, w * i:w * i + w]
def f(rng, *shape):
    return mx_ref.flush((rng.standard_normal(shape, dtype=np.float32) * np.exp2(rng.integers(-2, 3, shape[:-1] + (1,)))).astype(BF))
def wide(rng, *shape, cols=0):
    v = rng.standard_normal(shape, dtype=np.float32) * np.exp2(rng.integers(-12, 13, shape)).astype(np.float32)
    if cols: v *= np.repeat(np.exp2(rng.integers(-cols, cols + 1, shape[:-2] + (1, shape[-1] // 4))) * (rng.random(shape[:-2] + (1, shape[-1] // 4)) > 0.0625), 4, axis=-1).astype(np.float32)
    return mx_ref.flush(v.astype(BF))
T, S, CAPP, O = 256, 256, 64, 2
def counts(rng, zero=0.125, quiet=()):
    send = [r for r in range(N) if r not in quiet]
    n = np.zeros((N, N), int)
    for d in range(N): n[send[rng.integers(0, len(send))], d] = 16
    for k in rng.permutation(N * N):
        r, d = k // N, k % N
        if r in send and rng.random() > zero: n[r, d] += min(rng.integers(0, CAPP + 1), CAPP - n[r, d], T - n[r].sum(), S - n[:, d].sum())
    return n
def stored(n):
    return np.stack([table(np.concatenate([n[r], np.zeros(16 - N, int)])) for r in range(N)])
def setup_inputs(rng):
    return {"x": f(rng, N, 128, 4 * T), "cn": stored(counts(rng)), "w": f(rng, N, 128, 512 * O)}
def setup_inputs_full(rng):
    n = np.zeros((N, N), int); a, b = rng.permutation(N), rng.permutation(N)
    for i in range(N):
        for j in range(min(T // CAPP, S // CAPP, N)): n[a[i], b[(i + j) % N]] = CAPP
    return {**setup_inputs(rng), "cn": stored(n)}
def setup_inputs_none(rng):
    n = counts(rng, zero=0.6, quiet=(int(rng.integers(0, N)),)); n[:, rng.integers(0, N)] = 0
    return {**setup_inputs(rng), "cn": stored(n)}
def setup_inputs_skew(rng):
    n = rng.integers(0, 4, (N, N)); n[rng.integers(0, N, N), np.arange(N)] = 4
    d = rng.integers(0, N); n[:, d] = 0; n[(d + rng.integers(1, N)) % N, d] = CAPP
    while n[:, d].sum() < S:
        q = rng.integers(0, N)
        if n[q, d] < CAPP: n[q, d] += 1
    return {**setup_inputs(rng), "cn": stored(n)}
def setup_inputs_last(rng):
    n = np.zeros((N, N), int)
    for r in (N - 2, N - 1):
        n[r] = 1
        while n[r].sum() < T:
            q = rng.integers(0, N)
            if n[r, q] < CAPP: n[r, q] += 1
    return {**setup_inputs(rng), "cn": stored(n)}
def setup_inputs_spread(rng):
    d = setup_inputs(rng); d["x"] = wide(rng, N, 128, 4 * T, cols=8); return d
def check_inputs(d):
    b = []
    e = np.stack([entries(d["cn"][r]) for r in range(N)]).astype(np.int64); n = e[:, :N]
    if n.min() < 0 or n.max() > CAPP: b.append("count")
    if (e[:, N:] != 0).any(): b.append("zeros")
    if (n.sum(axis=1) > T).any(): b.append("sent")
    if (n.sum(axis=0) > S).any(): b.append("received")
    return b
def reference(x, cn, w):
    n = np.stack([entries(cn[r])[:N] for r in range(N)])
    y = np.zeros((N, 128, O * S), np.float32); ln = np.zeros((N, 1, N + 1), np.float32)
    for d in range(N):
        ln[d, 0, 1:] = np.add.accumulate(n[:, d])
        k = int(np.add.reduce(n[:, d])); t = np.zeros((128, 4 * S), BF); at = 0
        for s in range(N):
            a, m = int(np.add.reduce(n[s, :d])), int(n[s, d])
            t[:, 4 * at:4 * (at + m)] = x[s][:, 4 * a:4 * (a + m)]; at += m
        q = mx_ref.quantize(t)
        for o in range(O): y[d][:, S * o:S * o + k] = mx_ref.matmul(mx_ref.quantize(np.ascontiguousarray(cut(w[d], o))), q)[:, :k]
    return {"y": y, "ln": ln}

@@ -1,0 +1,299 @@
+from concourse.bass import DstId, RemoteDMATransfer
+from concourse.mybir import AluOpType, ActivationFunctionType, dt
+
+CAP = 64
+NR = 8
+NX = 256
+ZC = NR * CAP
+SG = NR + 1
+
+F8, U8, F32, I32, BF = "float8_e4m3fn_x4", "uint8", "float32", "int32", "bfloat16"
+SCRATCH = {name: ("sbuf", [p, n], d) for name, p, n, d in (
+    ("xt", 128, 4 * NX, BF), ("wt", 128, 1024, BF), ("zt", 128, 512, BF),
+    ("xq", 128, NX + 128, F8), ("xs", 128, NX + 128, U8),
+    ("wq", 128, 256, F8), ("wsc", 128, 256, U8),
+    ("sq", 128, 7 * CAP, F8), ("ss", 128, 7 * CAP, U8),
+    ("hq", 128, 2 * CAP, F8), ("hs", 128, 4 * CAP, U8), ("hc", 128, 1, I32),
+    ("lq", 128, ZC + 128, F8), ("ls", 128, ZC + 128, U8),
+    ("aq", 128, NX, F8), ("asc", 128, NX, U8),
+    ("cnr", 1, 16, I32), ("bc", 128, 8, I32), ("rc", 128, 32, I32),
+    ("pidx", 128, 1, I32), ("pmi", 128, 1, I32), ("pmf", 128, 1, F32), ("jj", 128, 16, F32), ("ii", 128, 16, F32),
+    ("cf", 128, 8, F32), ("pse", 128, 9, F32), ("lsend", 128, 28, "uint16"), ("lown", 128, 4, "uint16"),
+    ("rf", 128, 8, F32), ("pl", 128, 9, F32), ("dd", 128, 8, F32),
+    ("mk", 128, 16 * SG, F32), ("sg", 128, 16 * SG, F32), ("sc", 128, 16 * SG, F32), ("lrec", 128, 16, "uint16"),
+    ("ysb", 128, 512, F32))}
+SCRATCH["ps"] = ("psum", [128, 2048], F32)
+SEMAPHORES = ["v", "cnl", "xl", "wl", "gi", "bcd", "qx", "qw", "pcx", "pdx", "psx", "psd", "own", "owns", "pref", "ld", "lo",
+              "fa", "fb", "ga", "gb", "m0a", "m1a", "m0b", "m1b", "s0", "s1", "v0", "v1", "lnd", "yd", "zd",
+              "sent", "cnt", "cod", "sca", "hci", "hqi", "hsi", "lr"]
+
+
+def bits(engines):
+    return sum(1 << e for e in engines)
+
+
+def share(engines, n):
+    k = 1
+    while 2 * k * n <= len(engines):
+        k *= 2
+    return [engines[i * k:(i + 1) * k] for i in range(n)]
+
+
+def plan(core_r, T, topo):
+    cores = T.cores
+    r = T.rank_of(core_r)
+    turn = [(r + k) % NR for k in range(1, NR)]
+    direct = [d for d in turn if topo.may_write(core_r, cores[d])]
+    cross = [d for d in range(NR) if d != r and d not in direct]
+    mine = sorted(direct + [r]).index(r)
+    cross = cross[mine:] + cross[:mine]
+    relays = [h for h in topo.cores_of(core_r) if h != core_r and all(topo.may_write(h, cores[d]) for d in cross)]
+    far = [h for h in relays if topo.die(h) != topo.die(core_r)]
+    near = [h for h in relays if topo.die(h) == topo.die(core_r)]
+    return direct, cross, far, near
+
+
+def forwards(core_r, T, topo):
+    direct, cross, far, near = plan(core_r, T, topo)
+    out = {}
+    for k in range(2):
+        out[far[k]] = (cross[k], [("codes", i, cross[2 * k + i]) for i in range(2)])
+    out[near[0]] = (cross[2], [("scales", i, d) for i, d in enumerate(cross)])
+    out[near[1]] = (cross[3], [("scales", 1 + i, d) for i, d in enumerate(direct)])
+    return out
+
+
+def relay_engines(h, jobs, T, topo):
+    return share(topo.engines(h, T.cores[jobs[0][2]]), len(jobs))
+
+
+def hop_engines(core_r, T, topo):
+    direct, cross, far, near = plan(core_r, T, topo)
+    onc = topo.engines(core_r, far[0])
+    off = topo.engines(core_r, T.cores[direct[0]])
+    return share(onc, 2), share([e for e in onc if e not in off], 2)
+
+
+def arriving(rank, T, topo):
+    ncnt = ncod = nsca = 0
+    for s, c in enumerate(T.cores):
+        if s == rank:
+            continue
+        direct = plan(c, T, topo)[0]
+        if rank in direct:
+            off = topo.engines(c, T.cores[rank])
+            ncnt += len(share(off, len(direct))[0])
+            ncod += len(off)
+        for h, (cd, jobs) in forwards(c, T, topo).items():
+            if cd == rank:
+                ncnt += len(topo.engines(h, T.cores[rank]))
+            for (kind, slot, d), e in zip(jobs, relay_engines(h, jobs, T, topo)):
+                if d == rank and kind == "codes":
+                    ncod += len(e)
+                elif d == rank:
+                    nsca += len(e)
+    return ncnt, ncod, nsca
+
+
+def rank_program(g, core, T, topo):
+    rank = T.rank_of(core)
+    if rank is None:
+        for c in T.cores:
+            if core in topo.cores_of(c):
+                relay_program(g, core, c, T, topo)
+        return
+    ADD, GE, MULT, MIN, MAX = AluOpType.add, AluOpType.is_ge, AluOpType.mult, AluOpType.min, AluOpType.max
+    COPY = ActivationFunctionType.Copy
+    V, A, P, Y, S = g.vector, g.scalar, g.tensor, g.sync, T.sem
+    direct, cross, far, near = plan(core, T, topo)
+    order = cross + direct
+    w32 = dt.uint32
+
+    A.dma_start(T.xt[:], T.x[:]).then_inc(S.xl, 16)
+    Y.dma_start(T.cnr[0:1, 0:16], T.cn[:]).then_inc(S.cnl, 16)
+    Y.wait_ge(S.cnl, 16)
+    Y.dma_start(T.wt[:], T.w[:]).then_inc(S.wl, 16)
+
+    g.iota(T.pidx[:], [[1, 1]], 0, 1).then_inc(S.gi, 1)
+    g.iota(T.jj[:], [[16, 16]], 0, 0, allow_small_or_imprecise_dtypes=True).then_inc(S.gi, 1)
+    g.wait_ge(S.cnl, 16)
+    g.partition_broadcast(T.bc[:], T.cnr[0:1, 0:8], 128).then_inc(S.bcd, 1)
+    g.wait_ge(S.bcd, 1)
+    sent = [0]
+
+    def xfer(dst_core, dst, src, engines, sem):
+        rid, pid = topo.addr(dst_core, core)
+        sent[0] += len(engines)
+        return RemoteDMATransfer(dst_ids=[DstId(rid=rid, pnc=pid)], dma_engine_mask=bits(engines), remote_sem=sem,
+                                 srcs=[src], dsts=[dst])
+
+    off = topo.engines(core, T.cores[direct[0]])
+    onc = topo.engines(core, far[0])
+    work = forwards(core, T, topo)
+    g.remote_dma_fused([xfer(h, T.hc[:], T.bc[:, work[h][0]:work[h][0] + 1], e, S.hci)
+                        for h, e in zip(work, share(onc, len(work)))], local_sem=S.sent)
+    g.remote_dma_fused([xfer(T.cores[d], T.rc[:, 4 * rank:4 * rank + 1], T.bc[:, d:d + 1], e, S.cnt)
+                        for d, e in zip(direct, share(off, len(direct)))], local_sem=S.sent)
+
+    nv = [0]
+
+    def v(inst):
+        inst.then_inc(S.v, 1)
+        nv[0] += 1
+
+    def vw():
+        V.wait_ge(S.v, nv[0])
+
+    v(V.memset(T.zt[:], 0.0))
+    v(V.memset(T.pse[:, 0:1], 0.0))
+    V.wait_ge(S.gi, 2)
+    v(V.tensor_scalar(T.pmi[:], T.pidx[:], 15, None, AluOpType.bitwise_and))
+    vw()
+    v(V.quantize_mx(T.xq[:, NX:NX + 128], T.xs[:, NX:NX + 128], T.zt[:]))
+    v(V.tensor_copy(T.pmf[:], T.pmi[:]))
+    vw()
+    v(V.tensor_scalar(T.ii[:], T.jj[:], T.pmf[:], None, ADD))
+    V.wait_ge(S.bcd, 1)
+    v(V.tensor_copy(T.cf[:], T.bc[:]))
+    vw()
+    v(V.tensor_tensor_scan(T.pse[:, 1:9], T.cf[:], T.cf[:], 0.0, ADD, MAX))
+    vw()
+    for k, d in enumerate(order):
+        V.tensor_scalar(T.lsend[:, 4 * k:4 * k + 4], T.ii[:, 0:4], T.pse[:, d:d + 1], None, ADD).then_inc(S.ld, 1)
+    V.wait_ge(S.xl, 16)
+    V.quantize_mx(T.xq[:, 0:NX], T.xs[:, 0:NX], T.xt[:]).then_inc(S.qx, 1)
+    V.wait_ge(S.ld, len(order))
+    V.wait_ge(S.qx, 1)
+
+    nc = CAP * len(cross)
+    nd = CAP * len(direct)
+    win = NX + 128
+    cuts = [(0, nc, 0, nc // 16), (nc, nc + nd, nc // 16, (nc + nd) // 16)]
+    for (a, b, e, f), sem in zip(cuts, (S.pcx, S.pdx)):
+        V.tensor_copy(T.sq[:, a:b].bitcast(w32), T.xq[:, 0:win].bitcast(w32).indirect(T.lsend[:, e:f])).then_inc(sem, 1)
+    V.tensor_scalar(T.lown[:], T.ii[:, 0:4], T.pse[:, rank:rank + 1], None, ADD).then_inc(S.lo, 1)
+    v(V.tensor_copy(T.rc[:, 4 * rank:4 * rank + 1], T.bc[:, rank:rank + 1]))
+    V.wait_ge(S.lo, 1)
+    V.tensor_copy(T.lq[:, CAP * rank:CAP * rank + CAP].bitcast(w32),
+                  T.xq[:, 0:win].bitcast(w32).indirect(T.lown[:, 0:4])).then_inc(S.own, 1)
+    A.wait_ge(S.ld, len(order))
+    A.wait_ge(S.qx, 1)
+    for (a, b, e, f), sem in zip(cuts, (S.psx, S.psd)):
+        A.activation(T.ss[:, a:b], T.xs[:, 0:win].indirect(T.lsend[:, e:f]), COPY).then_inc(sem, 1)
+    A.wait_ge(S.lo, 1)
+    A.activation(T.ls[:, CAP * rank:CAP * rank + CAP], T.xs[:, 0:win].indirect(T.lown[:, 0:4]), COPY).then_inc(S.owns, 1)
+
+    hopc, hops = hop_engines(core, T, topo)
+    g.wait_ge(S.pcx, 1)
+    g.remote_dma_fused([xfer(far[k], T.hq[:].bitcast(dt.uint8), T.sq[:, 2 * CAP * k:2 * CAP * (k + 1)].bitcast(dt.uint8),
+                             hopc[k], S.hqi) for k in range(2)], local_sem=S.sent)
+    g.wait_ge(S.psx, 1)
+    g.wait_ge(S.psd, 1)
+    g.remote_dma_fused([xfer(near[k], T.hs[:], T.ss[:, 3 * CAP * k:3 * CAP * k + 4 * CAP], hops[k], S.hsi)
+                        for k in range(2)], local_sem=S.sent)
+    g.wait_ge(S.pdx, 1)
+    for k, d in enumerate(direct):
+        rid, pid = topo.addr(T.cores[d], core)
+        sent[0] += len(off)
+        g.remote_dma(T.lq[:, CAP * rank:CAP * rank + CAP].bitcast(dt.uint8),
+                     T.sq[:, nc + CAP * k:nc + CAP * k + CAP].bitcast(dt.uint8), S.cod, S.sent, pid, rid, bits(off))
+    g.wait_ge(S.sent, sent[0])
+
+    v(V.memset(T.pl[:, 0:1], 0.0))
+    v(V.memset(T.sg[:], 1.0))
+    v(V.quantize_mx(T.lq[:, ZC:ZC + 128], T.ls[:, ZC:ZC + 128], T.zt[:]))
+    v(V.tensor_scalar(T.mk[:, 0:16 * SG:SG], T.jj[:], T.pmf[:], None, ADD))
+    vw()
+    v(V.tensor_scalar(T.sg[:, 0:16 * SG:SG], T.jj[:], 0.0, None, MULT))
+    V.wait_ge(S.wl, 16)
+    V.quantize_mx(T.wq[:], T.wsc[:], T.wt[:]).then_inc(S.qw, 1)
+
+    ncnt, ncod, nsca = arriving(rank, T, topo)
+    vw()
+    V.wait_ge(S.cnt, ncnt)
+    v(V.tensor_copy(T.rf[:], T.rc[:, 0:32:4]))
+    v(V.tensor_scalar(T.dd[:], T.rc[:, 0:32:4], -1.0, float(CAP), MULT, ADD))
+    vw()
+    V.tensor_tensor_scan(T.pl[:, 1:9], T.rf[:], T.rf[:], 0.0, ADD, MAX).then_inc(S.pref, 1)
+    V.wait_ge(S.pref, 1)
+    for s in range(NR):
+        v(V.tensor_scalar(T.mk[:, 1 + s:16 * SG:SG], T.ii[:], T.pl[:, s + 1:s + 2], T.dd[:, s:s + 1], GE, MULT))
+    vw()
+    v(V.tensor_tensor_scan(T.sc[:], T.sg[:], T.mk[:], 0.0, MULT, ADD))
+    vw()
+    V.tensor_scalar(T.lrec[:], T.sc[:, NR:16 * SG:SG], float(ZC), None, MIN).then_inc(S.lr, 1)
+
+    Y.wait_ge(S.pref, 1)
+    Y.dma_start(T.ln[:], T.pl[0:1, 0:9]).then_inc(S.lnd, 16)
+
+    lw = ZC + 128
+    V.wait_ge(S.own, 1)
+    V.wait_ge(S.lr, 1)
+    V.wait_ge(S.cod, ncod)
+    for h, sem in enumerate((S.fa, S.fb)):
+        V.tensor_copy(T.aq[:, 128 * h:128 * h + 128].bitcast(w32),
+                      T.lq[:, 0:lw].bitcast(w32).indirect(T.lrec[:, 8 * h:8 * h + 8])).then_inc(sem, 1)
+    A.wait_ge(S.owns, 1)
+    A.wait_ge(S.lr, 1)
+    A.wait_ge(S.sca, nsca)
+    for h, sem in enumerate((S.ga, S.gb)):
+        A.activation(T.asc[:, 128 * h:128 * h + 128], T.ls[:, 0:lw].indirect(T.lrec[:, 8 * h:8 * h + 8]), COPY).then_inc(sem, 1)
+
+    P.wait_ge(S.qw, 1)
+    for h, (f1, g1, sems) in enumerate(((S.fa, S.ga, (S.m0a, S.m1a)), (S.fb, S.gb, (S.m0b, S.m1b)))):
+        P.wait_ge(f1, 1)
+        P.wait_ge(g1, 1)
+        for o in range(2):
+            bank = 512 * (2 * h + o)
+            P.matmul_mx(T.ps[:, bank:bank + 128], T.wq[:, 128 * o:128 * o + 128], T.wsc[:, 128 * o:128 * o + 128],
+                        T.aq[:, 128 * h:128 * h + 128], T.asc[:, 128 * h:128 * h + 128], True, True).then_inc(sems[o], 1)
+
+    for o, (m, s) in enumerate(((S.m0a, S.s0), (S.m1a, S.s1))):
+        A.wait_ge(m, 1)
+        A.activation(T.ysb[:, 256 * o:256 * o + 128], T.ps[:, 512 * o:512 * o + 128], COPY).then_inc(s, 1)
+    for o, (m, s) in enumerate(((S.m0b, S.v0), (S.m1b, S.v1))):
+        V.wait_ge(m, 1)
+        V.tensor_copy(T.ysb[:, 256 * o + 128:256 * o + 256], T.ps[:, 1024 + 512 * o:1024 + 512 * o + 128]).then_inc(s, 1)
+    Y.wait_ge(S.s0, 1)
+    Y.wait_ge(S.v0, 1)
+    Y.dma_start(T.y[:, 0:256], T.ysb[:, 0:256]).then_inc(S.yd, 16)
+    A.wait_ge(S.s1, 1)
+    A.wait_ge(S.v1, 1)
+    A.dma_start(T.y[:, 256:512], T.ysb[:, 256:512]).then_inc(S.zd, 16)
+    Y.wait_ge(S.yd, 16)
+    Y.wait_ge(S.lnd, 16)
+    A.wait_ge(S.zd, 16)
+    vw()
+
+
+def relay_program(g, core, home, T, topo):
+    work = forwards(home, T, topo)
+    if core not in work:
+        return
+    S = T.sem
+    src_rank = T.rank_of(home)
+    cd, jobs = work[core]
+    onc = topo.engines(home, core)
+    g.wait_ge(S.hci, len(share(onc, len(work))[0]))
+    dst = T.cores[cd]
+    rid, pid = topo.addr(dst, core)
+    eng = topo.engines(core, dst)
+    g.remote_dma(T.rc[:, 4 * src_rank:4 * src_rank + 1], T.hc[:], S.cnt, S.sent, pid, rid, bits(eng))
+    total = len(eng)
+    codes = jobs[0][0] == "codes"
+    hopc, hops = hop_engines(home, T, topo)
+    g.wait_ge(S.hqi if codes else S.hsi, len(hopc[0]) if codes else len(hops[0]))
+    tr = []
+    for (kind, slot, d), e in zip(jobs, relay_engines(core, jobs, T, topo)):
+        rid, pid = topo.addr(T.cores[d], core)
+        a, b = CAP * slot, CAP * slot + CAP
+        p, q = CAP * src_rank, CAP * src_rank + CAP
+        if codes:
+            src, dst, sem = T.hq[:, a:b].bitcast(dt.uint8), T.lq[:, p:q].bitcast(dt.uint8), S.cod
+        else:
+            src, dst, sem = T.hs[:, a:b], T.ls[:, p:q], S.sca
+        total += len(e)
+        tr.append(RemoteDMATransfer(dst_ids=[DstId(rid=rid, pnc=pid)], dma_engine_mask=bits(e), remote_sem=sem,
+                                    srcs=[src], dsts=[dst]))
+    g.remote_dma_fused(tr, local_sem=S.sent)
+    g.wait_ge(S.sent, total)

@@ -5,26 +5,32 @@ CAP = 64
 NR = 8
 NX = 256
 ZC = NR * CAP
-SG = NR + 1
+NE = 16 * NR
+PLAN = 3
 
-F8, U8, F32, I32, BF = "float8_e4m3fn_x4", "uint8", "float32", "int32", "bfloat16"
+F8, U8, F32, I32, BF, U16 = "float8_e4m3fn_x4", "uint8", "float32", "int32", "bfloat16", "uint16"
 SCRATCH = {name: ("sbuf", [p, n], d) for name, p, n, d in (
     ("xt", 128, 4 * NX, BF), ("wt", 128, 1024, BF), ("zt", 128, 512, BF),
-    ("xq", 128, NX + 128, F8), ("xs", 128, NX + 128, U8),
+    ("xq", 128, NX, F8), ("xs", 128, NX, U8),
     ("wq", 128, 256, F8), ("wsc", 128, 256, U8),
     ("sq", 128, 7 * CAP, F8), ("ss", 128, 7 * CAP, U8),
-    ("hq", 128, 2 * CAP, F8), ("hs", 128, 4 * CAP, U8), ("hc", 128, 1, I32),
-    ("lq", 128, ZC + 128, F8), ("ls", 128, ZC + 128, U8),
+    ("hq", 128, 2 * CAP, F8), ("hs", 128, 2 * CAP, U8),
+    ("lq", 128, ZC + NX, F8), ("ls", 128, ZC + NX, U8),
     ("aq", 128, NX, F8), ("asc", 128, NX, U8),
-    ("cnr", 1, 16, I32), ("bc", 128, 8, I32), ("rc", 128, 32, I32),
-    ("pidx", 128, 1, I32), ("pmi", 128, 1, I32), ("pmf", 128, 1, F32), ("jj", 128, 16, F32), ("ii", 128, 16, F32),
-    ("cf", 128, 8, F32), ("pse", 128, 9, F32), ("lsend", 128, 28, "uint16"), ("lown", 128, 4, "uint16"),
-    ("rf", 128, 8, F32), ("pl", 128, 9, F32), ("dd", 128, 8, F32),
-    ("mk", 128, 16 * SG, F32), ("sg", 128, 16 * SG, F32), ("sc", 128, 16 * SG, F32), ("lrec", 128, 16, "uint16"),
+    ("cnr", 1, 16, I32), ("fil", 2, 64, I32), ("bc", 128, 8, I32),
+    ("rc", 128, 32, I32), ("rb", 128, 8, I32),
+    ("pidx", 128, NR, I32), ("pmi", 128, 1, I32), ("pmf", 128, 1, F32),
+    ("inc", 128, 32, F32), ("sl", 128, 32, F32), ("lsend", 128, 32, U16),
+    ("jj", 128, NE, F32), ("iir", 128, NE, F32), ("ii", 128, 16, F32),
+    ("p8", 128, NR, I32), ("rep", 128, NR, U16), ("neg", 128, NR, F32), ("gap", 128, NR, F32), ("pl", 128, NR + 1, F32),
+    ("mk", 128, NE, F32), ("gpr", 128, NE, F32), ("sc", 128, NE, F32), ("lrec", 128, 16, U16),
     ("ysb", 128, 512, F32))}
+SCRATCH["cd"] = ("dram", [128 + 16, 1], I32)
+SCRATCH["hd"] = ("dram", [128, 1], I32)
 SCRATCH["ps"] = ("psum", [128, 2048], F32)
-SEMAPHORES = ["v", "cnl", "xl", "wl", "gi", "bcd", "qx", "qw", "pcx", "pdx", "psx", "psd", "own", "owns", "pref", "ld", "lo",
-              "fa", "fb", "ga", "gb", "m0a", "m1a", "m0b", "m1b", "s0", "s1", "v0", "v1", "lnd", "yd", "zd",
+SEMAPHORES = ["v", "a", "fi", "cnl", "cnd", "xa", "xl", "wl", "gi", "gj", "bcd", "rbd", "qx", "qw", "pq", "psc",
+              "own", "owns", "ownc", "pm", "gp", "ddd", "repd", "pref", "ld",
+              "fa", "fb", "ga", "gb", "m0a", "m1a", "m0b", "m1b", "s0", "s1", "lnd", "yd", "zd",
               "sent", "cnt", "cod", "sca", "hci", "hqi", "hsi", "lr"]
 
 
@@ -45,54 +51,95 @@ def plan(core_r, T, topo):
     turn = [(r + k) % NR for k in range(1, NR)]
     direct = [d for d in turn if topo.may_write(core_r, cores[d])]
     cross = [d for d in range(NR) if d != r and d not in direct]
-    mine = sorted(direct + [r]).index(r)
-    cross = cross[mine:] + cross[:mine]
-    relays = [h for h in topo.cores_of(core_r) if h != core_r and all(topo.may_write(h, cores[d]) for d in cross)]
+    others = [h for h in topo.cores_of(core_r) if h != core_r]
+    relays = [h for h in others if all(topo.may_write(h, cores[d]) for d in cross)]
     far = [h for h in relays if topo.die(h) != topo.die(core_r)]
     near = [h for h in relays if topo.die(h) == topo.die(core_r)]
-    return direct, cross, far, near
+    rest = [h for h in others if h not in relays]
+    pfar = [h for h in rest if topo.die(h) != topo.die(core_r)]
+    pnear = [h for h in rest if topo.die(h) == topo.die(core_r)]
+    return direct, cross, far, near, pfar, pnear
 
 
-def forwards(core_r, T, topo):
-    direct, cross, far, near = plan(core_r, T, topo)
-    out = {}
-    for k in range(2):
-        out[far[k]] = (cross[k], [("codes", i, cross[2 * k + i]) for i in range(2)])
-    out[near[0]] = (cross[2], [("scales", i, d) for i, d in enumerate(cross)])
-    out[near[1]] = (cross[3], [("scales", 1 + i, d) for i, d in enumerate(direct)])
+def calls(core_r, T, topo):
+    direct, cross, far, near, pfar, pnear = plan(core_r, T, topo)
+    onc = topo.engines(core_r, far[0])
+    off = topo.engines(core_r, T.cores[direct[0]])
+    inner = [e for e in onc if e not in off]
+
+    def call(kind, width, writes, engines):
+        return (kind, width, [w + (e,) for w, e in zip(writes, share(engines, len(writes)))])
+
+    def straight(k):
+        return (T.cores[direct[k]], 4 + k, [])
+
+    plain = pfar if PLAN == 3 else [pnear[0], pfar[0]]
+    mine = sorted(direct + [T.rank_of(core_r)]).index(T.rank_of(core_r))
+    ports = (far + near)[mine:] + (far + near)[:mine]
+    out = [call("count", 1, [(h, k, [k]) for h, k in zip(ports + plain, (0, 1, 2, 3, 5, 6))], inner),
+           call("count", 1, [straight(0)], off)]
+    if PLAN == 3:
+        out += [call("codes", 1, [(h, k, [k]) for k, h in enumerate(ports)], onc),
+                call("scales", 1, [(h, k, [k]) for k, h in enumerate(ports)], onc),
+                call("scales", 2, [(plain[0], 4, [4, 5]), (plain[1], 5, [6])], inner)]
+    else:
+        out += [call("codes", 2, [(h, 2 * k, [2 * k, 2 * k + 1]) for k, h in enumerate(far)], onc),
+                call("scales", 2, [(h, 2 * k, [2 * k, 2 * k + 1]) for k, h in enumerate(near)]
+                     + [(plain[0], 4, [4, 5]), (plain[1], 5, [6])], onc)]
+    out += [call("codes", 1, [straight(0), straight(1)], off), call("codes", 1, [straight(2)], off)]
     return out
 
 
-def relay_engines(h, jobs, T, topo):
-    return share(topo.engines(h, T.cores[jobs[0][2]]), len(jobs))
-
-
-def hop_engines(core_r, T, topo):
-    direct, cross, far, near = plan(core_r, T, topo)
-    onc = topo.engines(core_r, far[0])
-    off = topo.engines(core_r, T.cores[direct[0]])
-    return share(onc, 2), share([e for e in onc if e not in off], 2)
+def forwards(core_r, T, topo):
+    direct, cross = plan(core_r, T, topo)[:2]
+    order = cross + direct
+    out = {}
+    for kind, width, writes in calls(core_r, T, topo):
+        for h, first, on, e in writes:
+            if on:
+                eng = share(topo.engines(h, T.cores[order[on[0]]]), len(on))
+                out.setdefault(h, []).append((kind, len(e), [(k - first, order[k], f) for k, f in zip(on, eng)]))
+    return out
 
 
 def arriving(rank, T, topo):
-    ncnt = ncod = nsca = 0
-    for s, c in enumerate(T.cores):
-        if s == rank:
-            continue
-        direct = plan(c, T, topo)[0]
-        if rank in direct:
-            off = topo.engines(c, T.cores[rank])
-            ncnt += len(share(off, len(direct))[0])
-            ncod += len(off)
-        for h, (cd, jobs) in forwards(c, T, topo).items():
-            if cd == rank:
-                ncnt += len(topo.engines(h, T.cores[rank]))
-            for (kind, slot, d), e in zip(jobs, relay_engines(h, jobs, T, topo)):
-                if d == rank and kind == "codes":
-                    ncod += len(e)
-                elif d == rank:
-                    nsca += len(e)
-    return ncnt, ncod, nsca
+    n = {"count": 0, "codes": 0, "scales": 0}
+    for c in T.cores:
+        for kind, width, writes in calls(c, T, topo):
+            n[kind] += sum(len(e) for h, first, on, e in writes if h == T.cores[rank])
+        for jobs in forwards(c, T, topo).values():
+            for kind, inc, on in jobs:
+                n[kind] += sum(len(e) for slot, d, e in on if d == rank)
+    return n
+
+
+def runs(ranks):
+    out = []
+    for k, d in enumerate(ranks):
+        if out and d == out[-1][1] + out[-1][2]:
+            out[-1][2] += 1
+        else:
+            out.append([k, d, 1])
+    return out
+
+
+def landing(T, kind, src_rank):
+    p = CAP * src_rank
+    return {"count": (T.rc[:, 4 * src_rank:4 * src_rank + 1], T.sem.cnt),
+            "codes": (T.lq[:, p:p + CAP].bitcast(dt.uint8), T.sem.cod),
+            "scales": (T.ls[:, p:p + CAP], T.sem.sca)}[kind]
+
+
+def held(T, kind, a, n):
+    return {"count": (T.hd[:], T.sem.hci),
+            "codes": (T.hq[:, CAP * a:CAP * (a + n)].bitcast(dt.uint8), T.sem.hqi),
+            "scales": (T.hs[:, CAP * a:CAP * (a + n)], T.sem.hsi)}[kind]
+
+
+def transfer(topo, core, dst_core, dst, src, engines, sem):
+    rid, pid = topo.addr(dst_core, core)
+    return RemoteDMATransfer(dst_ids=[DstId(rid=rid, pnc=pid)], dma_engine_mask=bits(engines), remote_sem=sem,
+                             srcs=[src], dsts=[dst])
 
 
 def rank_program(g, core, T, topo):
@@ -102,38 +149,21 @@ def rank_program(g, core, T, topo):
             if core in topo.cores_of(c):
                 relay_program(g, core, c, T, topo)
         return
-    ADD, GE, MULT, MIN, MAX = AluOpType.add, AluOpType.is_ge, AluOpType.mult, AluOpType.min, AluOpType.max
-    COPY = ActivationFunctionType.Copy
+    ADD, MULT, MIN, MAX = AluOpType.add, AluOpType.mult, AluOpType.min, AluOpType.max
+    COPY, IDENT = ActivationFunctionType.Copy, ActivationFunctionType.Identity
     V, A, P, Y, S = g.vector, g.scalar, g.tensor, g.sync, T.sem
-    direct, cross, far, near = plan(core, T, topo)
+    direct, cross = plan(core, T, topo)[:2]
     order = cross + direct
     w32 = dt.uint32
 
-    A.dma_start(T.xt[:], T.x[:]).then_inc(S.xl, 16)
     Y.dma_start(T.cnr[0:1, 0:16], T.cn[:]).then_inc(S.cnl, 16)
-    Y.wait_ge(S.cnl, 16)
-    Y.dma_start(T.wt[:], T.w[:]).then_inc(S.wl, 16)
-
-    g.iota(T.pidx[:], [[1, 1]], 0, 1).then_inc(S.gi, 1)
-    g.iota(T.jj[:], [[16, 16]], 0, 0, allow_small_or_imprecise_dtypes=True).then_inc(S.gi, 1)
-    g.wait_ge(S.cnl, 16)
-    g.partition_broadcast(T.bc[:], T.cnr[0:1, 0:8], 128).then_inc(S.bcd, 1)
-    g.wait_ge(S.bcd, 1)
-    sent = [0]
-
-    def xfer(dst_core, dst, src, engines, sem):
-        rid, pid = topo.addr(dst_core, core)
-        sent[0] += len(engines)
-        return RemoteDMATransfer(dst_ids=[DstId(rid=rid, pnc=pid)], dma_engine_mask=bits(engines), remote_sem=sem,
-                                 srcs=[src], dsts=[dst])
-
-    off = topo.engines(core, T.cores[direct[0]])
-    onc = topo.engines(core, far[0])
-    work = forwards(core, T, topo)
-    g.remote_dma_fused([xfer(h, T.hc[:], T.bc[:, work[h][0]:work[h][0] + 1], e, S.hci)
-                        for h, e in zip(work, share(onc, len(work)))], local_sem=S.sent)
-    g.remote_dma_fused([xfer(T.cores[d], T.rc[:, 4 * rank:4 * rank + 1], T.bc[:, d:d + 1], e, S.cnt)
-                        for d, e in zip(direct, share(off, len(direct)))], local_sem=S.sent)
+    Y.dma_start(T.cd[0:16, :], T.cn[:]).then_inc(S.cnd, 16)
+    V.memset(T.fil[:], 0).then_inc(S.fi, 1)
+    A.dma_start(T.xt[:, 0:2 * NX], T.x[:, 0:2 * NX]).then_inc(S.xa, 16)
+    A.wait_ge(S.fi, 1)
+    A.dma_start(T.cd[16:144, :], T.fil[:]).then_inc(S.cnd, 16)
+    A.dma_start(T.xt[:, 2 * NX:4 * NX], T.x[:, 2 * NX:4 * NX]).then_inc(S.xl, 16)
+    A.dma_start(T.wt[:], T.w[:]).then_inc(S.wl, 16)
 
     nv = [0]
 
@@ -144,98 +174,112 @@ def rank_program(g, core, T, topo):
     def vw():
         V.wait_ge(S.v, nv[0])
 
-    v(V.memset(T.zt[:], 0.0))
-    v(V.memset(T.pse[:, 0:1], 0.0))
-    V.wait_ge(S.gi, 2)
-    v(V.tensor_scalar(T.pmi[:], T.pidx[:], 15, None, AluOpType.bitwise_and))
-    vw()
-    v(V.quantize_mx(T.xq[:, NX:NX + 128], T.xs[:, NX:NX + 128], T.zt[:]))
-    v(V.tensor_copy(T.pmf[:], T.pmi[:]))
-    vw()
-    v(V.tensor_scalar(T.ii[:], T.jj[:], T.pmf[:], None, ADD))
-    V.wait_ge(S.bcd, 1)
-    v(V.tensor_copy(T.cf[:], T.bc[:]))
-    vw()
-    v(V.tensor_tensor_scan(T.pse[:, 1:9], T.cf[:], T.cf[:], 0.0, ADD, MAX))
-    vw()
-    for k, d in enumerate(order):
-        V.tensor_scalar(T.lsend[:, 4 * k:4 * k + 4], T.ii[:, 0:4], T.pse[:, d:d + 1], None, ADD).then_inc(S.ld, 1)
-    V.wait_ge(S.xl, 16)
-    V.quantize_mx(T.xq[:, 0:NX], T.xs[:, 0:NX], T.xt[:]).then_inc(S.qx, 1)
-    V.wait_ge(S.ld, len(order))
-    V.wait_ge(S.qx, 1)
-
-    nc = CAP * len(cross)
-    nd = CAP * len(direct)
-    win = NX + 128
-    cuts = [(0, nc, 0, nc // 16), (nc, nc + nd, nc // 16, (nc + nd) // 16)]
-    for (a, b, e, f), sem in zip(cuts, (S.pcx, S.pdx)):
-        V.tensor_copy(T.sq[:, a:b].bitcast(w32), T.xq[:, 0:win].bitcast(w32).indirect(T.lsend[:, e:f])).then_inc(sem, 1)
-    V.tensor_scalar(T.lown[:], T.ii[:, 0:4], T.pse[:, rank:rank + 1], None, ADD).then_inc(S.lo, 1)
-    v(V.tensor_copy(T.rc[:, 4 * rank:4 * rank + 1], T.bc[:, rank:rank + 1]))
-    V.wait_ge(S.lo, 1)
-    V.tensor_copy(T.lq[:, CAP * rank:CAP * rank + CAP].bitcast(w32),
-                  T.xq[:, 0:win].bitcast(w32).indirect(T.lown[:, 0:4])).then_inc(S.own, 1)
-    A.wait_ge(S.ld, len(order))
-    A.wait_ge(S.qx, 1)
-    for (a, b, e, f), sem in zip(cuts, (S.psx, S.psd)):
-        A.activation(T.ss[:, a:b], T.xs[:, 0:win].indirect(T.lsend[:, e:f]), COPY).then_inc(sem, 1)
-    A.wait_ge(S.lo, 1)
-    A.activation(T.ls[:, CAP * rank:CAP * rank + CAP], T.xs[:, 0:win].indirect(T.lown[:, 0:4]), COPY).then_inc(S.owns, 1)
-
-    hopc, hops = hop_engines(core, T, topo)
-    g.wait_ge(S.pcx, 1)
-    g.remote_dma_fused([xfer(far[k], T.hq[:].bitcast(dt.uint8), T.sq[:, 2 * CAP * k:2 * CAP * (k + 1)].bitcast(dt.uint8),
-                             hopc[k], S.hqi) for k in range(2)], local_sem=S.sent)
-    g.wait_ge(S.psx, 1)
-    g.wait_ge(S.psd, 1)
-    g.remote_dma_fused([xfer(near[k], T.hs[:], T.ss[:, 3 * CAP * k:3 * CAP * k + 4 * CAP], hops[k], S.hsi)
-                        for k in range(2)], local_sem=S.sent)
-    g.wait_ge(S.pdx, 1)
-    for k, d in enumerate(direct):
-        rid, pid = topo.addr(T.cores[d], core)
-        sent[0] += len(off)
-        g.remote_dma(T.lq[:, CAP * rank:CAP * rank + CAP].bitcast(dt.uint8),
-                     T.sq[:, nc + CAP * k:nc + CAP * k + CAP].bitcast(dt.uint8), S.cod, S.sent, pid, rid, bits(off))
-    g.wait_ge(S.sent, sent[0])
-
+    v(V.memset(T.inc[:], 16.0))
     v(V.memset(T.pl[:, 0:1], 0.0))
-    v(V.memset(T.sg[:], 1.0))
-    v(V.quantize_mx(T.lq[:, ZC:ZC + 128], T.ls[:, ZC:ZC + 128], T.zt[:]))
-    v(V.tensor_scalar(T.mk[:, 0:16 * SG:SG], T.jj[:], T.pmf[:], None, ADD))
+    v(V.memset(T.neg[:], -float(CAP)))
+    V.wait_ge(S.gi, 1)
+    v(V.tensor_scalar(T.pmi[:], T.pidx[:, 0:1], 15, None, AluOpType.bitwise_and))
+    v(V.tensor_scalar(T.p8[:], T.pidx[:], NR - 1, None, AluOpType.bitwise_and))
     vw()
-    v(V.tensor_scalar(T.sg[:, 0:16 * SG:SG], T.jj[:], 0.0, None, MULT))
+    v(V.memset(T.inc[:, 0:1], 0.0))
+    V.tensor_copy(T.pmf[:], T.pmi[:]).then_inc(S.pm, 1)
+    V.tensor_scalar(T.rep[:], T.p8[:], -1.0, NR - 1.0, MULT, ADD).then_inc(S.repd, 1)
+    v(V.memset(T.zt[:], 0.0))
+    A.wait_ge(S.gj, 1)
+    A.wait_ge(S.pm, 1)
+    A.activation(T.iir[:], T.jj[:], IDENT, bias=T.pmf[:]).then_inc(S.a, 1)
+    A.wait_ge(S.a, 1)
+    A.activation(T.ii[:], T.iir[:, NR - 1:NE:NR], IDENT, bias=float(CAP)).then_inc(S.a, 1)
+    V.wait_ge(S.repd, 1)
+    V.wait_ge(S.cnl, 16)
+    V.tensor_copy(T.rc[0:1, 4 * rank:4 * rank + 1], T.cnr[0:1, rank:rank + 1]).then_inc(S.ownc, 1)
+    V.wait_ge(S.pm, 1)
+    vw()
+    V.wait_ge(S.xa, 16)
+    V.quantize_mx(T.xq[:, 0:128], T.xs[:, 0:128], T.xt[:, 0:2 * NX]).then_inc(S.qx, 1)
+    V.wait_ge(S.bcd, 1)
+    v(V.tensor_scalar(T.inc[:, 4:32:4], T.bc[:, 0:7], 16.0 - CAP, None, ADD))
+    vw()
+    v(V.tensor_tensor_scan(T.sl[:], T.inc[:], T.inc[:], T.pmf[:], ADD, MAX))
+    V.wait_ge(S.xl, 16)
+    V.quantize_mx(T.xq[:, 128:NX], T.xs[:, 128:NX], T.xt[:, 2 * NX:4 * NX]).then_inc(S.qx, 1)
+    vw()
+    V.tensor_scalar(T.lsend[:], T.sl[:], float(NX - 1), None, MIN).then_inc(S.ld, 1)
+    V.wait_ge(S.ld, 1)
+    V.wait_ge(S.qx, 2)
+
+    picks = runs(cross) + [(len(cross) + k, d, n) for k, d, n in runs(direct)]
+    for k, d, n in picks:
+        V.tensor_copy(T.sq[:, CAP * k:CAP * (k + n)].bitcast(w32),
+                      T.xq[:].bitcast(w32).indirect(T.lsend[:, 4 * d:4 * (d + n)])).then_inc(S.pq, 1)
+    V.tensor_copy(T.lq[:, CAP * rank:CAP * rank + CAP].bitcast(w32),
+                  T.xq[:].bitcast(w32).indirect(T.lsend[:, 4 * rank:4 * rank + 4])).then_inc(S.own, 1)
+    A.wait_ge(S.ld, 1)
+    A.wait_ge(S.qx, 2)
+    for k, d, n in picks:
+        A.activation(T.ss[:, CAP * k:CAP * (k + n)], T.xs[:].indirect(T.lsend[:, 4 * d:4 * (d + n)]), COPY).then_inc(S.psc, 1)
+    A.activation(T.ls[:, CAP * rank:CAP * rank + CAP], T.xs[:].indirect(T.lsend[:, 4 * rank:4 * rank + 4]),
+                 COPY).then_inc(S.owns, 1)
+
+    g.iota(T.pidx[:], [[0, NR]], 0, 1).then_inc(S.gi, 1)
+    g.iota(T.jj[:], [[16, 16], [CAP, NR]], -ZC, 0, allow_small_or_imprecise_dtypes=True).then_inc(S.gj, 1)
+    g.wait_ge(S.cnl, 16)
+    g.partition_broadcast(T.bc[:], T.cnr[0:1, 0:8], 128).then_inc(S.bcd, 1)
+    g.wait_ge(S.cnd, 32)
+    sent = 0
+    for kind, width, writes in calls(core, T, topo):
+        if kind != "count":
+            last = max(first + width for h, first, on, e in writes)
+            g.wait_ge(S.pq if kind == "codes" else S.psc, len([k for k, d, n in picks if k < last]))
+        tr = []
+        for h, first, on, e in writes:
+            a, b = CAP * first, CAP * (first + width)
+            src = {"count": T.cd[order[first]:order[first] + 128, :], "codes": T.sq[:, a:b].bitcast(dt.uint8),
+                   "scales": T.ss[:, a:b]}[kind]
+            dst, sem = held(T, kind, 0, width) if on else landing(T, kind, rank)
+            tr.append(transfer(topo, core, h, dst, src, e, sem))
+            sent += len(e)
+        g.remote_dma_fused(tr, local_sem=S.sent)
+    arr = arriving(rank, T, topo)
+    g.wait_ge(S.ownc, 1)
+    g.wait_ge(S.cnt, arr["count"])
+    g.partition_broadcast(T.rb[:], T.rc[0:1, 0:32:4], 128).then_inc(S.rbd, 1)
+    g.wait_ge(S.sent, sent)
+
+    for a in range(ZC, ZC + NX, 128):
+        v(V.quantize_mx(T.lq[:, a:a + 128], T.ls[:, a:a + 128], T.zt[:]))
     V.wait_ge(S.wl, 16)
     V.quantize_mx(T.wq[:], T.wsc[:], T.wt[:]).then_inc(S.qw, 1)
 
-    ncnt, ncod, nsca = arriving(rank, T, topo)
+    V.wait_ge(S.a, 2)
     vw()
-    V.wait_ge(S.cnt, ncnt)
-    v(V.tensor_copy(T.rf[:], T.rc[:, 0:32:4]))
-    v(V.tensor_scalar(T.dd[:], T.rc[:, 0:32:4], -1.0, float(CAP), MULT, ADD))
+    V.wait_ge(S.rbd, 1)
+    V.tensor_tensor_scan(T.gap[:], T.rb[:], T.neg[:], 0.0, ADD, ADD).then_inc(S.gp, 1)
+    V.wait_ge(S.gp, 1)
+    v(V.tensor_tensor(T.mk[:], T.gap[:].indirect(T.rep[:]), T.iir[:], AluOpType.is_le))
+    V.tensor_tensor_scan(T.pl[:, 1:9], T.rb[:], T.rb[:], 0.0, ADD, MAX).then_inc(S.pref, 1)
+    A.wait_ge(S.repd, 1)
+    A.wait_ge(S.gp, 1)
+    A.activation(T.gpr[:], T.gap[:].indirect(T.rep[:]), COPY).then_inc(S.ddd, 1)
     vw()
-    V.tensor_tensor_scan(T.pl[:, 1:9], T.rf[:], T.rf[:], 0.0, ADD, MAX).then_inc(S.pref, 1)
-    V.wait_ge(S.pref, 1)
-    for s in range(NR):
-        v(V.tensor_scalar(T.mk[:, 1 + s:16 * SG:SG], T.ii[:], T.pl[:, s + 1:s + 2], T.dd[:, s:s + 1], GE, MULT))
+    V.wait_ge(S.ddd, 1)
+    v(V.tensor_tensor_scan(T.sc[:], T.gpr[:], T.mk[:], 0.0, MIN, MULT))
     vw()
-    v(V.tensor_tensor_scan(T.sc[:], T.sg[:], T.mk[:], 0.0, MULT, ADD))
-    vw()
-    V.tensor_scalar(T.lrec[:], T.sc[:, NR:16 * SG:SG], float(ZC), None, MIN).then_inc(S.lr, 1)
+    V.tensor_tensor(T.lrec[:], T.ii[:], T.sc[:, NR - 1:NE:NR], AluOpType.subtract).then_inc(S.lr, 1)
 
     Y.wait_ge(S.pref, 1)
     Y.dma_start(T.ln[:], T.pl[0:1, 0:9]).then_inc(S.lnd, 16)
 
-    lw = ZC + 128
+    lw = ZC + NX
     V.wait_ge(S.own, 1)
+    V.wait_ge(S.cod, arr["codes"])
     V.wait_ge(S.lr, 1)
-    V.wait_ge(S.cod, ncod)
     for h, sem in enumerate((S.fa, S.fb)):
         V.tensor_copy(T.aq[:, 128 * h:128 * h + 128].bitcast(w32),
                       T.lq[:, 0:lw].bitcast(w32).indirect(T.lrec[:, 8 * h:8 * h + 8])).then_inc(sem, 1)
     A.wait_ge(S.owns, 1)
+    A.wait_ge(S.sca, arr["scales"])
     A.wait_ge(S.lr, 1)
-    A.wait_ge(S.sca, nsca)
     for h, sem in enumerate((S.ga, S.gb)):
         A.activation(T.asc[:, 128 * h:128 * h + 128], T.ls[:, 0:lw].indirect(T.lrec[:, 8 * h:8 * h + 8]), COPY).then_inc(sem, 1)
 
@@ -248,52 +292,32 @@ def rank_program(g, core, T, topo):
             P.matmul_mx(T.ps[:, bank:bank + 128], T.wq[:, 128 * o:128 * o + 128], T.wsc[:, 128 * o:128 * o + 128],
                         T.aq[:, 128 * h:128 * h + 128], T.asc[:, 128 * h:128 * h + 128], True, True).then_inc(sems[o], 1)
 
-    for o, (m, s) in enumerate(((S.m0a, S.s0), (S.m1a, S.s1))):
-        A.wait_ge(m, 1)
-        A.activation(T.ysb[:, 256 * o:256 * o + 128], T.ps[:, 512 * o:512 * o + 128], COPY).then_inc(s, 1)
-    for o, (m, s) in enumerate(((S.m0b, S.v0), (S.m1b, S.v1))):
-        V.wait_ge(m, 1)
-        V.tensor_copy(T.ysb[:, 256 * o + 128:256 * o + 256], T.ps[:, 1024 + 512 * o:1024 + 512 * o + 128]).then_inc(s, 1)
-    Y.wait_ge(S.s0, 1)
-    Y.wait_ge(S.v0, 1)
-    Y.dma_start(T.y[:, 0:256], T.ysb[:, 0:256]).then_inc(S.yd, 16)
-    A.wait_ge(S.s1, 1)
-    A.wait_ge(S.v1, 1)
-    A.dma_start(T.y[:, 256:512], T.ysb[:, 256:512]).then_inc(S.zd, 16)
-    Y.wait_ge(S.yd, 16)
+    for h, (m0, m1) in enumerate(((S.m0a, S.m1a), (S.m0b, S.m1b))):
+        V.wait_ge(m0, 1)
+        V.tensor_copy(T.ysb[:, 128 * h:128 * h + 128], T.ps[:, 1024 * h:1024 * h + 128]).then_inc(S.s0, 1)
+        A.wait_ge(m1, 1)
+        A.activation(T.ysb[:, 256 + 128 * h:256 + 128 * h + 128], T.ps[:, 1024 * h + 512:1024 * h + 640],
+                     COPY).then_inc(S.s1, 1)
+    for a, sem, n in ((0, S.s0, 1), (256, S.s1, 1), (128, S.s0, 2)):
+        Y.wait_ge(sem, n)
+        Y.dma_start(T.y[:, a:a + 128], T.ysb[:, a:a + 128]).then_inc(S.yd, 16)
+    A.wait_ge(S.s1, 2)
+    A.dma_start(T.y[:, 384:512], T.ysb[:, 384:512]).then_inc(S.zd, 16)
+    Y.wait_ge(S.yd, 48)
     Y.wait_ge(S.lnd, 16)
     A.wait_ge(S.zd, 16)
     vw()
 
 
 def relay_program(g, core, home, T, topo):
-    work = forwards(home, T, topo)
-    if core not in work:
-        return
-    S = T.sem
-    src_rank = T.rank_of(home)
-    cd, jobs = work[core]
-    onc = topo.engines(home, core)
-    g.wait_ge(S.hci, len(share(onc, len(work))[0]))
-    dst = T.cores[cd]
-    rid, pid = topo.addr(dst, core)
-    eng = topo.engines(core, dst)
-    g.remote_dma(T.rc[:, 4 * src_rank:4 * src_rank + 1], T.hc[:], S.cnt, S.sent, pid, rid, bits(eng))
-    total = len(eng)
-    codes = jobs[0][0] == "codes"
-    hopc, hops = hop_engines(home, T, topo)
-    g.wait_ge(S.hqi if codes else S.hsi, len(hopc[0]) if codes else len(hops[0]))
-    tr = []
-    for (kind, slot, d), e in zip(jobs, relay_engines(core, jobs, T, topo)):
-        rid, pid = topo.addr(T.cores[d], core)
-        a, b = CAP * slot, CAP * slot + CAP
-        p, q = CAP * src_rank, CAP * src_rank + CAP
-        if codes:
-            src, dst, sem = T.hq[:, a:b].bitcast(dt.uint8), T.lq[:, p:q].bitcast(dt.uint8), S.cod
-        else:
-            src, dst, sem = T.hs[:, a:b], T.ls[:, p:q], S.sca
-        total += len(e)
-        tr.append(RemoteDMATransfer(dst_ids=[DstId(rid=rid, pnc=pid)], dma_engine_mask=bits(e), remote_sem=sem,
-                                    srcs=[src], dsts=[dst]))
-    g.remote_dma_fused(tr, local_sem=S.sent)
-    g.wait_ge(S.sent, total)
+    total = 0
+    for kind, inc, on in forwards(home, T, topo).get(core, []):
+        g.wait_ge(held(T, kind, 0, 1)[1], inc)
+        tr = []
+        for slot, d, e in on:
+            dst, sem = landing(T, kind, T.rank_of(home))
+            tr.append(transfer(topo, core, T.cores[d], dst, held(T, kind, slot, 1)[0], e, sem))
+            total += len(e)
+        g.remote_dma_fused(tr, local_sem=T.sem.sent)
+    if total:
+        g.wait_ge(T.sem.sent, total)

from concourse.bass import DstId, RemoteDMATransfer
from concourse.mybir import AluOpType, ActivationFunctionType, dt

CAP = 64
NR = 8
NX = 256
ZC = NR * CAP
NE = 16 * NR
PLAN = 3

F8, U8, F32, I32, BF, U16 = "float8_e4m3fn_x4", "uint8", "float32", "int32", "bfloat16", "uint16"
SCRATCH = {name: ("sbuf", [p, n], d) for name, p, n, d in (
    ("xt", 128, 4 * NX, BF), ("wt", 128, 1024, BF), ("zt", 128, 512, BF),
    ("xq", 128, NX, F8), ("xs", 128, NX, U8),
    ("wq", 128, 256, F8), ("wsc", 128, 256, U8),
    ("sq", 128, 7 * CAP, F8), ("ss", 128, 7 * CAP, U8),
    ("hq", 128, 2 * CAP, F8), ("hs", 128, 2 * CAP, U8),
    ("lq", 128, ZC + NX, F8), ("ls", 128, ZC + NX, U8),
    ("aq", 128, NX, F8), ("asc", 128, NX, U8),
    ("cnr", 1, 16, I32), ("fil", 2, 64, I32), ("bc", 128, 8, I32),
    ("rc", 128, 32, I32), ("rb", 128, 8, I32),
    ("pidx", 128, NR, I32), ("pmi", 128, 1, I32), ("pmf", 128, 1, F32),
    ("inc", 128, 32, F32), ("sl", 128, 32, F32), ("lsend", 128, 32, U16),
    ("jj", 128, NE, F32), ("iir", 128, NE, F32), ("ii", 128, 16, F32),
    ("p8", 128, NR, I32), ("rep", 128, NR, U16), ("neg", 128, NR, F32), ("gap", 128, NR, F32), ("pl", 128, NR + 1, F32),
    ("mk", 128, NE, F32), ("gpr", 128, NE, F32), ("sc", 128, NE, F32), ("lrec", 128, 16, U16),
    ("ysb", 128, 512, F32))}
SCRATCH["cd"] = ("dram", [128 + 16, 1], I32)
SCRATCH["hd"] = ("dram", [128, 1], I32)
SCRATCH["ps"] = ("psum", [128, 2048], F32)
SEMAPHORES = ["v", "a", "fi", "cnl", "cnd", "xa", "xl", "wl", "gi", "gj", "bcd", "rbd", "qx", "qw", "pq", "psc",
              "own", "owns", "ownc", "pm", "gp", "ddd", "repd", "pref", "ld",
              "fa", "fb", "ga", "gb", "m0a", "m1a", "m0b", "m1b", "s0", "s1", "lnd", "yd", "zd",
              "sent", "cnt", "cod", "sca", "hci", "hqi", "hsi", "lr"]


def bits(engines):
    return sum(1 << e for e in engines)


def share(engines, n):
    k = 1
    while 2 * k * n <= len(engines):
        k *= 2
    return [engines[i * k:(i + 1) * k] for i in range(n)]


def plan(core_r, T, topo):
    cores = T.cores
    r = T.rank_of(core_r)
    turn = [(r + k) % NR for k in range(1, NR)]
    direct = [d for d in turn if topo.may_write(core_r, cores[d])]
    cross = [d for d in range(NR) if d != r and d not in direct]
    others = [h for h in topo.cores_of(core_r) if h != core_r]
    relays = [h for h in others if all(topo.may_write(h, cores[d]) for d in cross)]
    far = [h for h in relays if topo.die(h) != topo.die(core_r)]
    near = [h for h in relays if topo.die(h) == topo.die(core_r)]
    rest = [h for h in others if h not in relays]
    pfar = [h for h in rest if topo.die(h) != topo.die(core_r)]
    pnear = [h for h in rest if topo.die(h) == topo.die(core_r)]
    return direct, cross, far, near, pfar, pnear


def calls(core_r, T, topo):
    direct, cross, far, near, pfar, pnear = plan(core_r, T, topo)
    onc = topo.engines(core_r, far[0])
    off = topo.engines(core_r, T.cores[direct[0]])
    inner = [e for e in onc if e not in off]

    def call(kind, width, writes, engines):
        return (kind, width, [w + (e,) for w, e in zip(writes, share(engines, len(writes)))])

    def straight(k):
        return (T.cores[direct[k]], 4 + k, [])

    plain = pfar if PLAN == 3 else [pnear[0], pfar[0]]
    mine = sorted(direct + [T.rank_of(core_r)]).index(T.rank_of(core_r))
    ports = (far + near)[mine:] + (far + near)[:mine]
    out = [call("count", 1, [(h, k, [k]) for h, k in zip(ports + plain, (0, 1, 2, 3, 5, 6))], inner),
           call("count", 1, [straight(0)], off)]
    if PLAN == 3:
        out += [call("codes", 1, [(h, k, [k]) for k, h in enumerate(ports)], onc),
                call("scales", 1, [(h, k, [k]) for k, h in enumerate(ports)], onc),
                call("scales", 2, [(plain[0], 4, [4, 5]), (plain[1], 5, [6])], inner)]
    else:
        out += [call("codes", 2, [(h, 2 * k, [2 * k, 2 * k + 1]) for k, h in enumerate(far)], onc),
                call("scales", 2, [(h, 2 * k, [2 * k, 2 * k + 1]) for k, h in enumerate(near)]
                     + [(plain[0], 4, [4, 5]), (plain[1], 5, [6])], onc)]
    out += [call("codes", 1, [straight(0), straight(1)], off), call("codes", 1, [straight(2)], off)]
    return out


def forwards(core_r, T, topo):
    direct, cross = plan(core_r, T, topo)[:2]
    order = cross + direct
    out = {}
    for kind, width, writes in calls(core_r, T, topo):
        for h, first, on, e in writes:
            if on:
                eng = share(topo.engines(h, T.cores[order[on[0]]]), len(on))
                out.setdefault(h, []).append((kind, len(e), [(k - first, order[k], f) for k, f in zip(on, eng)]))
    return out


def arriving(rank, T, topo):
    n = {"count": 0, "codes": 0, "scales": 0}
    for c in T.cores:
        for kind, width, writes in calls(c, T, topo):
            n[kind] += sum(len(e) for h, first, on, e in writes if h == T.cores[rank])
        for jobs in forwards(c, T, topo).values():
            for kind, inc, on in jobs:
                n[kind] += sum(len(e) for slot, d, e in on if d == rank)
    return n


def runs(ranks):
    out = []
    for k, d in enumerate(ranks):
        if out and d == out[-1][1] + out[-1][2]:
            out[-1][2] += 1
        else:
            out.append([k, d, 1])
    return out


def landing(T, kind, src_rank):
    p = CAP * src_rank
    return {"count": (T.rc[:, 4 * src_rank:4 * src_rank + 1], T.sem.cnt),
            "codes": (T.lq[:, p:p + CAP].bitcast(dt.uint8), T.sem.cod),
            "scales": (T.ls[:, p:p + CAP], T.sem.sca)}[kind]


def held(T, kind, a, n):
    return {"count": (T.hd[:], T.sem.hci),
            "codes": (T.hq[:, CAP * a:CAP * (a + n)].bitcast(dt.uint8), T.sem.hqi),
            "scales": (T.hs[:, CAP * a:CAP * (a + n)], T.sem.hsi)}[kind]


def transfer(topo, core, dst_core, dst, src, engines, sem):
    rid, pid = topo.addr(dst_core, core)
    return RemoteDMATransfer(dst_ids=[DstId(rid=rid, pnc=pid)], dma_engine_mask=bits(engines), remote_sem=sem,
                             srcs=[src], dsts=[dst])


def rank_program(g, core, T, topo):
    rank = T.rank_of(core)
    if rank is None:
        for c in T.cores:
            if core in topo.cores_of(c):
                relay_program(g, core, c, T, topo)
        return
    ADD, MULT, MIN, MAX = AluOpType.add, AluOpType.mult, AluOpType.min, AluOpType.max
    COPY, IDENT = ActivationFunctionType.Copy, ActivationFunctionType.Identity
    V, A, P, Y, S = g.vector, g.scalar, g.tensor, g.sync, T.sem
    direct, cross = plan(core, T, topo)[:2]
    order = cross + direct
    w32 = dt.uint32

    Y.dma_start(T.cnr[0:1, 0:16], T.cn[:]).then_inc(S.cnl, 16)
    Y.dma_start(T.cd[0:16, :], T.cn[:]).then_inc(S.cnd, 16)
    V.memset(T.fil[:], 0).then_inc(S.fi, 1)
    A.dma_start(T.xt[:, 0:2 * NX], T.x[:, 0:2 * NX]).then_inc(S.xa, 16)
    A.wait_ge(S.fi, 1)
    A.dma_start(T.cd[16:144, :], T.fil[:]).then_inc(S.cnd, 16)
    A.dma_start(T.xt[:, 2 * NX:4 * NX], T.x[:, 2 * NX:4 * NX]).then_inc(S.xl, 16)
    A.dma_start(T.wt[:], T.w[:]).then_inc(S.wl, 16)

    nv = [0]

    def v(inst):
        inst.then_inc(S.v, 1)
        nv[0] += 1

    def vw():
        V.wait_ge(S.v, nv[0])

    v(V.memset(T.inc[:], 16.0))
    v(V.memset(T.pl[:, 0:1], 0.0))
    v(V.memset(T.neg[:], -float(CAP)))
    V.wait_ge(S.gi, 1)
    v(V.tensor_scalar(T.pmi[:], T.pidx[:, 0:1], 15, None, AluOpType.bitwise_and))
    v(V.tensor_scalar(T.p8[:], T.pidx[:], NR - 1, None, AluOpType.bitwise_and))
    vw()
    v(V.memset(T.inc[:, 0:1], 0.0))
    V.tensor_copy(T.pmf[:], T.pmi[:]).then_inc(S.pm, 1)
    V.tensor_scalar(T.rep[:], T.p8[:], -1.0, NR - 1.0, MULT, ADD).then_inc(S.repd, 1)
    v(V.memset(T.zt[:], 0.0))
    A.wait_ge(S.gj, 1)
    A.wait_ge(S.pm, 1)
    A.activation(T.iir[:], T.jj[:], IDENT, bias=T.pmf[:]).then_inc(S.a, 1)
    A.wait_ge(S.a, 1)
    A.activation(T.ii[:], T.iir[:, NR - 1:NE:NR], IDENT, bias=float(CAP)).then_inc(S.a, 1)
    V.wait_ge(S.repd, 1)
    V.wait_ge(S.cnl, 16)
    V.tensor_copy(T.rc[0:1, 4 * rank:4 * rank + 1], T.cnr[0:1, rank:rank + 1]).then_inc(S.ownc, 1)
    V.wait_ge(S.pm, 1)
    vw()
    V.wait_ge(S.xa, 16)
    V.quantize_mx(T.xq[:, 0:128], T.xs[:, 0:128], T.xt[:, 0:2 * NX]).then_inc(S.qx, 1)
    V.wait_ge(S.bcd, 1)
    v(V.tensor_scalar(T.inc[:, 4:32:4], T.bc[:, 0:7], 16.0 - CAP, None, ADD))
    vw()
    v(V.tensor_tensor_scan(T.sl[:], T.inc[:], T.inc[:], T.pmf[:], ADD, MAX))
    V.wait_ge(S.xl, 16)
    V.quantize_mx(T.xq[:, 128:NX], T.xs[:, 128:NX], T.xt[:, 2 * NX:4 * NX]).then_inc(S.qx, 1)
    vw()
    V.tensor_scalar(T.lsend[:], T.sl[:], float(NX - 1), None, MIN).then_inc(S.ld, 1)
    V.wait_ge(S.ld, 1)
    V.wait_ge(S.qx, 2)

    picks = runs(cross) + [(len(cross) + k, d, n) for k, d, n in runs(direct)]
    for k, d, n in picks:
        V.tensor_copy(T.sq[:, CAP * k:CAP * (k + n)].bitcast(w32),
                      T.xq[:].bitcast(w32).indirect(T.lsend[:, 4 * d:4 * (d + n)])).then_inc(S.pq, 1)
    V.tensor_copy(T.lq[:, CAP * rank:CAP * rank + CAP].bitcast(w32),
                  T.xq[:].bitcast(w32).indirect(T.lsend[:, 4 * rank:4 * rank + 4])).then_inc(S.own, 1)
    A.wait_ge(S.ld, 1)
    A.wait_ge(S.qx, 2)
    for k, d, n in picks:
        A.activation(T.ss[:, CAP * k:CAP * (k + n)], T.xs[:].indirect(T.lsend[:, 4 * d:4 * (d + n)]), COPY).then_inc(S.psc, 1)
    A.activation(T.ls[:, CAP * rank:CAP * rank + CAP], T.xs[:].indirect(T.lsend[:, 4 * rank:4 * rank + 4]),
                 COPY).then_inc(S.owns, 1)

    g.iota(T.pidx[:], [[0, NR]], 0, 1).then_inc(S.gi, 1)
    g.iota(T.jj[:], [[16, 16], [CAP, NR]], -ZC, 0, allow_small_or_imprecise_dtypes=True).then_inc(S.gj, 1)
    g.wait_ge(S.cnl, 16)
    g.partition_broadcast(T.bc[:], T.cnr[0:1, 0:8], 128).then_inc(S.bcd, 1)
    g.wait_ge(S.cnd, 32)
    sent = 0
    for kind, width, writes in calls(core, T, topo):
        if kind != "count":
            last = max(first + width for h, first, on, e in writes)
            g.wait_ge(S.pq if kind == "codes" else S.psc, len([k for k, d, n in picks if k < last]))
        tr = []
        for h, first, on, e in writes:
            a, b = CAP * first, CAP * (first + width)
            src = {"count": T.cd[order[first]:order[first] + 128, :], "codes": T.sq[:, a:b].bitcast(dt.uint8),
                   "scales": T.ss[:, a:b]}[kind]
            dst, sem = held(T, kind, 0, width) if on else landing(T, kind, rank)
            tr.append(transfer(topo, core, h, dst, src, e, sem))
            sent += len(e)
        g.remote_dma_fused(tr, local_sem=S.sent)
    arr = arriving(rank, T, topo)
    g.wait_ge(S.ownc, 1)
    g.wait_ge(S.cnt, arr["count"])
    g.partition_broadcast(T.rb[:], T.rc[0:1, 0:32:4], 128).then_inc(S.rbd, 1)
    g.wait_ge(S.sent, sent)

    for a in range(ZC, ZC + NX, 128):
        v(V.quantize_mx(T.lq[:, a:a + 128], T.ls[:, a:a + 128], T.zt[:]))
    V.wait_ge(S.wl, 16)
    V.quantize_mx(T.wq[:], T.wsc[:], T.wt[:]).then_inc(S.qw, 1)

    V.wait_ge(S.a, 2)
    vw()
    V.wait_ge(S.rbd, 1)
    V.tensor_tensor_scan(T.gap[:], T.rb[:], T.neg[:], 0.0, ADD, ADD).then_inc(S.gp, 1)
    V.wait_ge(S.gp, 1)
    v(V.tensor_tensor(T.mk[:], T.gap[:].indirect(T.rep[:]), T.iir[:], AluOpType.is_le))
    V.tensor_tensor_scan(T.pl[:, 1:9], T.rb[:], T.rb[:], 0.0, ADD, MAX).then_inc(S.pref, 1)
    A.wait_ge(S.repd, 1)
    A.wait_ge(S.gp, 1)
    A.activation(T.gpr[:], T.gap[:].indirect(T.rep[:]), COPY).then_inc(S.ddd, 1)
    vw()
    V.wait_ge(S.ddd, 1)
    v(V.tensor_tensor_scan(T.sc[:], T.gpr[:], T.mk[:], 0.0, MIN, MULT))
    vw()
    V.tensor_tensor(T.lrec[:], T.ii[:], T.sc[:, NR - 1:NE:NR], AluOpType.subtract).then_inc(S.lr, 1)

    Y.wait_ge(S.pref, 1)
    Y.dma_start(T.ln[:], T.pl[0:1, 0:9]).then_inc(S.lnd, 16)

    lw = ZC + NX
    V.wait_ge(S.own, 1)
    V.wait_ge(S.cod, arr["codes"])
    V.wait_ge(S.lr, 1)
    for h, sem in enumerate((S.fa, S.fb)):
        V.tensor_copy(T.aq[:, 128 * h:128 * h + 128].bitcast(w32),
                      T.lq[:, 0:lw].bitcast(w32).indirect(T.lrec[:, 8 * h:8 * h + 8])).then_inc(sem, 1)
    A.wait_ge(S.owns, 1)
    A.wait_ge(S.sca, arr["scales"])
    A.wait_ge(S.lr, 1)
    for h, sem in enumerate((S.ga, S.gb)):
        A.activation(T.asc[:, 128 * h:128 * h + 128], T.ls[:, 0:lw].indirect(T.lrec[:, 8 * h:8 * h + 8]), COPY).then_inc(sem, 1)

    P.wait_ge(S.qw, 1)
    for h, (f1, g1, sems) in enumerate(((S.fa, S.ga, (S.m0a, S.m1a)), (S.fb, S.gb, (S.m0b, S.m1b)))):
        P.wait_ge(f1, 1)
        P.wait_ge(g1, 1)
        for o in range(2):
            bank = 512 * (2 * h + o)
            P.matmul_mx(T.ps[:, bank:bank + 128], T.wq[:, 128 * o:128 * o + 128], T.wsc[:, 128 * o:128 * o + 128],
                        T.aq[:, 128 * h:128 * h + 128], T.asc[:, 128 * h:128 * h + 128], True, True).then_inc(sems[o], 1)

    for h, (m0, m1) in enumerate(((S.m0a, S.m1a), (S.m0b, S.m1b))):
        V.wait_ge(m0, 1)
        V.tensor_copy(T.ysb[:, 128 * h:128 * h + 128], T.ps[:, 1024 * h:1024 * h + 128]).then_inc(S.s0, 1)
        A.wait_ge(m1, 1)
        A.activation(T.ysb[:, 256 + 128 * h:256 + 128 * h + 128], T.ps[:, 1024 * h + 512:1024 * h + 640],
                     COPY).then_inc(S.s1, 1)
    for a, sem, n in ((0, S.s0, 1), (256, S.s1, 1), (128, S.s0, 2)):
        Y.wait_ge(sem, n)
        Y.dma_start(T.y[:, a:a + 128], T.ysb[:, a:a + 128]).then_inc(S.yd, 16)
    A.wait_ge(S.s1, 2)
    A.dma_start(T.y[:, 384:512], T.ysb[:, 384:512]).then_inc(S.zd, 16)
    Y.wait_ge(S.yd, 48)
    Y.wait_ge(S.lnd, 16)
    A.wait_ge(S.zd, 16)
    vw()


def relay_program(g, core, home, T, topo):
    total = 0
    for kind, inc, on in forwards(home, T, topo).get(core, []):
        g.wait_ge(held(T, kind, 0, 1)[1], inc)
        tr = []
        for slot, d, e in on:
            dst, sem = landing(T, kind, T.rank_of(home))
            tr.append(transfer(topo, core, T.cores[d], dst, held(T, kind, slot, 1)[0], e, sem))
            total += len(e)
        g.remote_dma_fused(tr, local_sem=T.sem.sent)
    if total:
        g.wait_ge(T.sem.sent, total)
